import numpy as np
import ml_dtypes


def mxq(x, axis, fmt="e4m3"):
    dtype, down = {"e4m3": (ml_dtypes.float8_e4m3fn, 7), "e5m2": (ml_dtypes.float8_e5m2, 14)}[fmt]
    v = np.moveaxis(np.asarray(x, np.float32).astype(ml_dtypes.bfloat16).astype(np.float64), axis, -1)
    blocks = v.reshape(v.shape[:-1] + (-1, 32))
    amax = np.abs(blocks).max(-1, keepdims=True)
    byte = np.maximum(np.where(amax > 0, np.frexp(amax)[1] - 1 + 127, 0) - down, 1)
    scale = np.exp2(byte - 127.0)
    codes = (blocks / scale).astype(np.float32).astype(dtype).astype(np.float64)
    return np.moveaxis((codes * scale).reshape(v.shape), -1, axis)


WIDE = False


def mx_kscale(k):
    if not WIDE:
        return np.ones(k)
    levels = np.array([10, -10, 5, -5, 0])
    if k % 512:
        return np.exp2(np.random.permutation(np.resize(levels, k // 32))).repeat(32)
    a = np.empty((k // 512, 16))
    for p in range(k // 512):
        a[p, :8] = np.random.permutation(np.resize(levels, 8))
        for g in range(8):
            far = levels[np.abs(levels - a[p, g]) >= 10]
            a[p, g + 8] = far[np.random.randint(len(far))]
    return np.exp2(a.ravel()).repeat(32)


def f64(x):
    return np.asarray(x).astype(np.float64)


def striped(idx):
    return np.tile(idx.reshape(-1, 16).T, (8, 1)).astype(np.uint16)


def unstriped(offs):
    return offs[:16].T.reshape(-1).astype(np.int64)


E2M1 = np.array([0.0, 0.5, 1.0, 1.5, 2.0, 3.0, 4.0, 6.0, -0.0, -0.5, -1.0, -1.5, -2.0, -3.0, -4.0, -6.0])


def pack_fp4(w):
    k, n = w.shape
    w = f64(np.asarray(w, np.float32).astype(ml_dtypes.bfloat16)).reshape(k // 32, 32, n)
    amax = np.abs(w).max(1)
    mant, ex = np.frexp(amax / 6.0)
    byte = np.clip(np.where(amax > 0, np.where(mant > 0.5, ex, ex - 1) + 127, 1), 1, 254)
    scaled = (w * np.exp2(127.0 - byte)[:, None, :]).reshape(k, n).astype(np.float32)
    c = np.ascontiguousarray(scaled.reshape(k // 512, 128, 4, n).transpose(0, 1, 3, 2)).astype(ml_dtypes.float4_e2m1fn).view(np.uint8) & 0xF
    words = (c[..., 0::2] | (c[..., 1::2] << 4)).reshape(k // 512, 128, 2 * n)
    return np.ascontiguousarray(words), np.ascontiguousarray(byte.astype(np.uint8).reshape(k // 512, 16, n))


def unpack_fp4(words, scales):
    g, _, n = scales.shape
    words = np.ascontiguousarray(words).reshape(g, 128, n, 2)
    nib = np.empty((g, 128, n, 4), np.uint8)
    nib[..., 0::2] = words & 0xF
    nib[..., 1::2] = words >> 4
    vals = E2M1[nib] * np.repeat(np.exp2(scales.astype(np.float64) - 127.0), 8, axis=1)[..., None]
    return vals.transpose(0, 1, 3, 2).reshape(g * 512, n)


def silu(v):
    return v / (1.0 + np.exp(-np.maximum(v, -700.0)))


K, T, S, D, V, H, N = 512, 1024, 512, 4, 256, 512, 256
P = 2 ** 7


def setup_inputs():
    n = np.random.standard_normal
    s = mx_kscale(K)[:, None]
    u = mx_kscale(H)
    packed_w2 = pack_fp4(n((H, N)) / np.sqrt(H) / u[:, None])
    return {
        "xT": (n((K, T)) * s).astype(np.float32),
        "w1": (n((K, H)) / np.sqrt(K) / s * u).astype(np.float32),
        "w2_words": packed_w2[0],
        "w2_scales": packed_w2[1],
        "gate": (np.tile(np.random.uniform(0.2, 1.0, (D, 1, V)) / np.sqrt(D), (1, P, 1))).astype(np.float32),
        "offs": striped(np.random.permutation(T)[:S]),
        "cen": striped(np.random.permutation(S)[:V]),
        "pos1": striped(np.random.permutation(S)[:V]),
        "pos2": striped(np.random.permutation(S)[:V]),
        "pos3": striped(np.random.permutation(S)[:V]),
        "pos4": striped(np.random.permutation(S)[:V]),
    }


def reference(xT, w1, w2_words, w2_scales, gate, offs, cen, pos1, pos2, pos3, pos4):
    xq = mxq(f64(xT)[:, unstriped(offs)], 0, "e4m3")
    h = silu(mxq(f64(w1), 0, "e4m3").T @ xq)
    z = h[:, unstriped(cen)] - (h[:, unstriped(pos1)] * f64(gate)[0, :1] + h[:, unstriped(pos2)] * f64(gate)[1, :1] + h[:, unstriped(pos3)] * f64(gate)[2, :1] + h[:, unstriped(pos4)] * f64(gate)[3, :1])
    return unpack_fp4(w2_words, w2_scales).T @ mxq(z, 0, "e4m3")

@@ -1,0 +1,232 @@
+from contextlib import ExitStack
+
+import concourse.mybir as mybir
+from concourse.masks import make_identity
+
+K, T, S, D, V, H, N = 512, 1024, 512, 4, 256, 512, 256
+FLOPS = 2 * K * H * S + 2 * H * N * V
+
+F32 = mybir.dt.float32
+BF16 = mybir.dt.bfloat16
+I32 = mybir.dt.int32
+U32 = mybir.dt.uint32
+U16 = mybir.dt.uint16
+U8 = mybir.dt.uint8
+FP8X4 = mybir.dt.float8_e4m3fn_x4
+FP4X4 = mybir.dt.float4_e2m1fn_x4
+MULT = mybir.AluOpType.mult
+SILU = mybir.ActivationFunctionType.Silu
+COPY = mybir.ActivationFunctionType.Copy
+
+P = 128
+X_CHUNKS = ((0, 512, "scalar"), (512, 896, "vector"), (896, 1024, "scalar"))
+
+
+def tile_picked_lapl_silu_e_kernel(
+    tc, xT, w1, w2_words, w2_scales, gate, offs, cen, pos1, pos2, pos3, pos4, out
+):
+    nc = tc.nc
+
+    def move(engine, dst, src):
+        if engine == "scalar":
+            nc.scalar.copy(dst, src)
+        else:
+            nc.vector.tensor_copy(dst, src)
+
+    with ExitStack() as ctx:
+        keep = ctx.enter_context(tc.tile_pool(name="keep", bufs=1))
+        ring = ctx.enter_context(tc.tile_pool(name="ring", bufs=6))
+        psum = ctx.enter_context(tc.psum_pool(name="psum", bufs=2))
+
+        def load_list(name, ap):
+            tile = keep.tile(list(ap.shape), U16, name=name)
+            nc.sync.dma_start(tile[:], ap)
+            return tile
+
+        warm = keep.tile([P, 8], F32, name="warm")
+        warm_out = keep.tile([P, 8], F32, name="warm_out")
+        nc.vector.memset(warm[:], 0.0)
+        nc.scalar.activation(warm_out[:], warm[:], SILU)
+
+        ident = keep.tile([P, P], F32, name="ident")
+        make_identity(nc, ident[:])
+        minus_one = keep.tile([P, V], F32, name="minus_one")
+        nc.vector.memset(minus_one[:], -1.0)
+        w2_sc = keep.tile([P, N], U8, name="w2_sc", align_bytes=64)
+        nc.vector.memset(w2_sc[:].bitcast(I32), 0)
+
+        x_view = xT.rearrange("(p u e) t -> p u e t", u=2, e=2)
+        x_raw = {}
+        offs_t = None
+        for u in range(2):
+            for c0, c1, eng in X_CHUNKS:
+                raw = keep.tile([P, 2, c1 - c0], F32, name=f"x_raw{u}_{c0}")
+                nc.sync.dma_start(raw[:], x_view[:, u, :, c0:c1])
+                x_raw[u, c0] = raw
+                if offs_t is None:
+                    offs_t = load_list("offs", offs)
+        w1_view = w1.rearrange("(p j) h -> p j h", j=4)
+        w1_a = keep.tile([P, 4, 2 * P], F32, name="w1_a")
+        nc.sync.dma_start(w1_a[:], w1_view[:, :, 0 : 2 * P])
+        cen_t = load_list("cen", cen)
+        gate_all = keep.tile([P, D, V], F32, name="gate_all")
+        nc.sync.dma_start(gate_all[:], gate.rearrange("d p v -> p d v"))
+        gate_t = [gate_all[:, d, :] for d in range(D)]
+        pos_t = [load_list("pos1", pos1)]
+        w1_b = keep.tile([P, 4, 2 * P], F32, name="w1_b")
+        nc.sync.dma_start(w1_b[:], w1_view[:, :, 2 * P : H])
+        pos_t.extend(load_list(name, ap) for name, ap in (("pos2", pos2), ("pos3", pos3), ("pos4", pos4)))
+        w2_w = keep.tile([P, 2 * N], U8, name="w2_w", align_bytes=64)
+        nc.sync.dma_start(w2_w[:].bitcast(I32), w2_words[0].bitcast(I32))
+        for q in range(4):
+            nc.sync.dma_start(
+                w2_sc[32 * q : 32 * q + 4, :].bitcast(I32), w2_scales[0, 4 * q : 4 * q + 4, :].bitcast(I32)
+            )
+
+        picked = keep.tile([P, S, 2], U32, name="picked", align_bytes=64)
+        pairs = []
+        for u in range(2):
+            pr = keep.tile([P, T], U32, name=f"pairs{u}", align_bytes=64)
+            pr_bf = pr[:].bitcast(BF16)
+            for c0, c1, eng in X_CHUNKS:
+                move(
+                    eng,
+                    pr_bf[:, 2 * c0 : 2 * c1].rearrange("p (c i e) -> p c e i", i=4, e=2),
+                    x_raw[u, c0][:].rearrange("p e (c i) -> p c e i", i=4),
+                )
+            pairs.append(pr)
+            if u == 0:
+                nc.vector.tensor_copy(picked[:, :, 0], pr[:].indirect(offs_t[:]))
+
+        w1_bf = []
+        w1_codes = keep.tile([P, H], U32, name="w1_codes", align_bytes=64)
+        w1_sc = keep.tile([P, H], U8, name="w1_sc", align_bytes=64)
+
+        def cast_w1(c):
+            src = (w1_a, w1_b)[c // 2][:, :, P * (c % 2) : P * (c % 2 + 1)]
+            return src.rearrange("p j (c i) -> p c j i", i=4)
+
+        def quant_w1(c0, c1):
+            bf = keep.tile([P, 4 * P * (c1 - c0)], BF16, name=f"w1_bf{c0}", align_bytes=64)
+            for c in range(c0, c1):
+                nc.scalar.copy(
+                    bf[:, 4 * P * (c - c0) : 4 * P * (c - c0 + 1)].rearrange("p (c i j) -> p c j i", i=4, j=4),
+                    cast_w1(c),
+                )
+            nc.vector.quantize_mx(
+                out=w1_codes[:, P * c0 : P * c1].bitcast(FP8X4), scales=w1_sc[:, P * c0 : P * c1], in_=bf[:]
+            )
+
+        x_codes = keep.tile([P, S], U32, name="x_codes", align_bytes=64)
+        x_sc = keep.tile([P, S], U8, name="x_sc", align_bytes=64)
+        picked_bf = picked[:].rearrange("p s u -> p (s u)").bitcast(BF16)
+        pieces = ((0, 256), (256, 384), (384, 512))
+
+        def gather_x(i):
+            s0, s1 = pieces[i]
+            nc.vector.tensor_copy(picked[:, s0:s1, 1], pairs[1][:].indirect(offs_t[:, s0 // 16 : s1 // 16]))
+
+        def quant_x(i):
+            s0, s1 = pieces[i]
+            nc.vector.quantize_mx(
+                out=x_codes[:, s0:s1].bitcast(FP8X4),
+                scales=x_sc[:, s0:s1],
+                in_=picked_bf[:, 4 * s0 : 4 * s1],
+            )
+
+        gather_x(0)
+        gather_x(1)
+        quant_x(0)
+        gather_x(2)
+        quant_w1(0, 1)
+        quant_x(1)
+        quant_x(2)
+
+        h_t = [keep.tile([P, S], F32, name=f"h{c}") for c in range(4)]
+
+        def first_layer(c, s0, s1):
+            acc = psum.tile([P, s1 - s0], F32, name="acc", tag="mm")
+            nc.tensor.matmul_mx(
+                out=acc[:],
+                lhsT=w1_codes[:, P * c : P * (c + 1)].bitcast(FP8X4),
+                lhsT_scale=w1_sc[:, P * c : P * (c + 1)],
+                rhs=x_codes[:, s0:s1].bitcast(FP8X4),
+                rhs_scale=x_sc[:, s0:s1],
+                start=True,
+                stop=True,
+            )
+            nc.scalar.activation(h_t[c][:, s0:s1], acc[:], SILU)
+
+        z_bf = [keep.tile([P, 2, P, 2], BF16, name=f"z_bf{g}") for g in range(2)]
+        lists = [cen_t] + pos_t
+        factors = [minus_one[:]] + gate_t
+
+        def laplacian(c, groups, engines):
+            v0, v1 = P * groups[0], P * (groups[-1] + 1)
+            sums = {g: psum.tile([P, P], F32, name=f"sum{g}", tag=f"sum{g}") for g in groups}
+            for d in range(D + 1):
+                term = ring.tile([P, v1 - v0], F32, name="term")
+                nc.vector.tensor_tensor(
+                    term[:], h_t[c][:].indirect(lists[d][:, v0 // 16 : v1 // 16]), factors[d][:, v0:v1], MULT
+                )
+                for g in groups:
+                    nc.tensor.matmul(
+                        sums[g][:],
+                        lhsT=term[:, P * g - v0 : P * (g + 1) - v0],
+                        rhs=ident[:],
+                        is_transpose=True,
+                        start=(d == 0),
+                        stop=(d == D),
+                    )
+            for g, eng in zip(groups, engines):
+                dst = z_bf[g][:, :, 32 * c : 32 * (c + 1), :]
+                src = sums[g][:].rearrange("v (q u e) -> v u q e", u=2, e=2)
+                if eng == "scalar":
+                    nc.scalar.activation(dst, src, COPY, scale=-1.0)
+                else:
+                    nc.vector.tensor_scalar_mul(dst, src, -1.0)
+
+        def second_layer(g, engines):
+            words = z_bf[g][:].rearrange("v u q e -> v (u q e)").bitcast(F32)
+            turned = psum.tile([P, 2, P], F32, name="turned", tag=f"sum{g}")
+            for u in range(2):
+                nc.tensor.transpose(turned[:, u, :], words[:, P * u : P * (u + 1)], ident[:])
+            z_in = keep.tile([P, P, 2], F32, name=f"z_in{g}", align_bytes=64)
+            move(engines[0], z_in[:], turned[:].rearrange("p u v -> p v u"))
+            z_codes = keep.tile([P, P], U32, name=f"z_codes{g}", align_bytes=64)
+            z_sc = keep.tile([P, P], U8, name=f"z_sc{g}", align_bytes=64)
+            nc.vector.quantize_mx(
+                out=z_codes[:].bitcast(FP8X4),
+                scales=z_sc[:],
+                in_=z_in[:].rearrange("p v u -> p (v u)").bitcast(BF16),
+            )
+            for m in range(2):
+                acc = psum.tile([P, P], F32, name="acc", tag="mm")
+                nc.tensor.matmul_mx(
+                    out=acc[:],
+                    lhsT=w2_w[:, 2 * P * m : 2 * P * (m + 1)].bitcast(FP4X4),
+                    lhsT_scale=w2_sc[:, P * m : P * (m + 1)],
+                    rhs=z_codes[:].bitcast(FP8X4),
+                    rhs_scale=z_sc[:],
+                    start=True,
+                    stop=True,
+                )
+                res = keep.tile([P, P], F32, name=f"res{g}{m}")
+                move(engines[1 + m], res[:], acc[:])
+                queue = nc.sync if m == 0 else nc.scalar
+                queue.dma_start(out[P * m : P * (m + 1), P * g : P * (g + 1)], res[:])
+
+        for s0, s1 in pieces:
+            first_layer(0, s0, s1)
+        quant_w1(1, 2)
+        first_layer(1, 0, S)
+        laplacian(0, (0, 1), ("scalar", "scalar"))
+        quant_w1(2, 4)
+        first_layer(2, 0, S)
+        first_layer(3, 0, S)
+        laplacian(1, (0, 1), ("scalar", "scalar"))
+        laplacian(2, (0, 1), ("scalar", "scalar"))
+        laplacian(3, (0,), ("scalar",))
+        laplacian(3, (1,), ("scalar",))
+        second_layer(0, ("scalar", "scalar", "scalar"))
+        second_layer(1, ("scalar", "vector", "scalar"))

@@ -19,7 +19,11 @@ SILU = mybir.ActivationFunctionType.Silu
 COPY = mybir.ActivationFunctionType.Copy
 
 P = 128
-X_CHUNKS = ((0, 512, "scalar"), (512, 896, "vector"), (896, 1024, "scalar"))
+X_CHUNKS = (
+    ((0, 640, "scalar"), (640, 1024, "vector")),
+    ((0, 384, "scalar"), (384, 768, "scalar"), (768, 1024, "vector")),
+)
+W1_CHUNKS = ((0, 1), (1, 2), (2, 4))
 
 
 def tile_picked_lapl_silu_e_kernel(
@@ -35,8 +39,7 @@ def tile_picked_lapl_silu_e_kernel(
 
     with ExitStack() as ctx:
         keep = ctx.enter_context(tc.tile_pool(name="keep", bufs=1))
-        ring = ctx.enter_context(tc.tile_pool(name="ring", bufs=6))
-        psum = ctx.enter_context(tc.psum_pool(name="psum", bufs=2))
+        psum = ctx.enter_context(tc.psum_pool(name="psum", bufs=1))
 
         def load_list(name, ap):
             tile = keep.tile(list(ap.shape), U16, name=name)
@@ -59,23 +62,30 @@ def tile_picked_lapl_silu_e_kernel(
         x_raw = {}
         offs_t = None
         for u in range(2):
-            for c0, c1, eng in X_CHUNKS:
+            for c0, c1, eng in X_CHUNKS[u]:
                 raw = keep.tile([P, 2, c1 - c0], F32, name=f"x_raw{u}_{c0}")
                 nc.sync.dma_start(raw[:], x_view[:, u, :, c0:c1])
                 x_raw[u, c0] = raw
                 if offs_t is None:
                     offs_t = load_list("offs", offs)
         w1_view = w1.rearrange("(p j) h -> p j h", j=4)
-        w1_a = keep.tile([P, 4, 2 * P], F32, name="w1_a")
-        nc.sync.dma_start(w1_a[:], w1_view[:, :, 0 : 2 * P])
+        w1_raw = {}
+
+        def load_w1(c0, c1):
+            raw = keep.tile([P, 4, P * (c1 - c0)], F32, name=f"w1_raw{c0}", tag=f"w1_raw{c0}")
+            nc.sync.dma_start(raw[:], w1_view[:, :, P * c0 : P * c1])
+            for c in range(c0, c1):
+                w1_raw[c] = raw[:, :, P * (c - c0) : P * (c - c0 + 1)]
+
+        load_w1(0, 1)
+        load_w1(1, 2)
         cen_t = load_list("cen", cen)
+        pos_t = [load_list("pos1", pos1)]
         gate_all = keep.tile([P, D, V], F32, name="gate_all")
         nc.sync.dma_start(gate_all[:], gate.rearrange("d p v -> p d v"))
         gate_t = [gate_all[:, d, :] for d in range(D)]
-        pos_t = [load_list("pos1", pos1)]
-        w1_b = keep.tile([P, 4, 2 * P], F32, name="w1_b")
-        nc.sync.dma_start(w1_b[:], w1_view[:, :, 2 * P : H])
         pos_t.extend(load_list(name, ap) for name, ap in (("pos2", pos2), ("pos3", pos3), ("pos4", pos4)))
+        load_w1(2, 4)
         w2_w = keep.tile([P, 2 * N], U8, name="w2_w", align_bytes=64)
         nc.sync.dma_start(w2_w[:].bitcast(I32), w2_words[0].bitcast(I32))
         for q in range(4):
@@ -86,9 +96,9 @@ def tile_picked_lapl_silu_e_kernel(
         picked = keep.tile([P, S, 2], U32, name="picked", align_bytes=64)
         pairs = []
         for u in range(2):
-            pr = keep.tile([P, T], U32, name=f"pairs{u}", align_bytes=64)
+            pr = keep.tile([P, T], U32, name=f"pairs{u}", tag=f"pairs{u}", align_bytes=64)
             pr_bf = pr[:].bitcast(BF16)
-            for c0, c1, eng in X_CHUNKS:
+            for c0, c1, eng in X_CHUNKS[u]:
                 move(
                     eng,
                     pr_bf[:, 2 * c0 : 2 * c1].rearrange("p (c i e) -> p c e i", i=4, e=2),
@@ -103,51 +113,43 @@ def tile_picked_lapl_silu_e_kernel(
         w1_sc = keep.tile([P, H], U8, name="w1_sc", align_bytes=64)
 
         def cast_w1(c):
-            src = (w1_a, w1_b)[c // 2][:, :, P * (c % 2) : P * (c % 2 + 1)]
+            src = w1_raw[c]
             return src.rearrange("p j (c i) -> p c j i", i=4)
 
-        def quant_w1(c0, c1):
-            bf = keep.tile([P, 4 * P * (c1 - c0)], BF16, name=f"w1_bf{c0}", align_bytes=64)
+        def quant_w1(c0, c1, bf):
             for c in range(c0, c1):
                 nc.scalar.copy(
                     bf[:, 4 * P * (c - c0) : 4 * P * (c - c0 + 1)].rearrange("p (c i j) -> p c j i", i=4, j=4),
                     cast_w1(c),
                 )
             nc.vector.quantize_mx(
-                out=w1_codes[:, P * c0 : P * c1].bitcast(FP8X4), scales=w1_sc[:, P * c0 : P * c1], in_=bf[:]
+                out=w1_codes[:, P * c0 : P * c1].bitcast(FP8X4), scales=w1_sc[:, P * c0 : P * c1], in_=bf
             )
 
         x_codes = keep.tile([P, S], U32, name="x_codes", align_bytes=64)
         x_sc = keep.tile([P, S], U8, name="x_sc", align_bytes=64)
         picked_bf = picked[:].rearrange("p s u -> p (s u)").bitcast(BF16)
-        pieces = ((0, 256), (256, 384), (384, 512))
-
-        def gather_x(i):
-            s0, s1 = pieces[i]
-            nc.vector.tensor_copy(picked[:, s0:s1, 1], pairs[1][:].indirect(offs_t[:, s0 // 16 : s1 // 16]))
-
-        def quant_x(i):
-            s0, s1 = pieces[i]
+        pieces = [(s0, s0 + S // 2) for s0 in range(0, S, S // 2)]
+        nc.vector.tensor_copy(picked[:, :, 1], pairs[1][:].indirect(offs_t[:]))
+        w1_first = keep.tile([P, 4 * P], BF16, name="w1_first", align_bytes=64)
+        quant_w1(0, 1, w1_first[:])
+        for s0, s1 in pieces:
             nc.vector.quantize_mx(
                 out=x_codes[:, s0:s1].bitcast(FP8X4),
                 scales=x_sc[:, s0:s1],
                 in_=picked_bf[:, 4 * s0 : 4 * s1],
             )
 
-        gather_x(0)
-        gather_x(1)
-        quant_x(0)
-        gather_x(2)
-        quant_w1(0, 1)
-        quant_x(1)
-        quant_x(2)
+        w1_second = keep.tile([P, 4 * P], BF16, name="w1_second", align_bytes=64)
+        quant_w1(1, 2, w1_second[:])
+        h_t = [keep.tile([P, S], F32, name=f"h{c}", tag="w1_raw1" if c == 0 else f"h{c}") for c in range(4)]
 
-        h_t = [keep.tile([P, S], F32, name=f"h{c}") for c in range(4)]
+        banks = [psum.tile([P, S], F32, name=f"bank{b}") for b in range(3)]
 
-        def first_layer(c, s0, s1):
-            acc = psum.tile([P, s1 - s0], F32, name="acc", tag="mm")
+        def first_layer(c, s0, s1, bank):
+            acc = banks[bank][:, 0 : s1 - s0]
             nc.tensor.matmul_mx(
-                out=acc[:],
+                out=acc,
                 lhsT=w1_codes[:, P * c : P * (c + 1)].bitcast(FP8X4),
                 lhsT_scale=w1_sc[:, P * c : P * (c + 1)],
                 rhs=x_codes[:, s0:s1].bitcast(FP8X4),
@@ -155,40 +157,37 @@ def tile_picked_lapl_silu_e_kernel(
                 start=True,
                 stop=True,
             )
-            nc.scalar.activation(h_t[c][:, s0:s1], acc[:], SILU)
+            nc.scalar.activation(h_t[c][:, s0:s1], acc, SILU)
 
         z_bf = [keep.tile([P, 2, P, 2], BF16, name=f"z_bf{g}") for g in range(2)]
         lists = [cen_t] + pos_t
         factors = [minus_one[:]] + gate_t
 
-        def laplacian(c, groups, engines):
+        def laplacian(c, groups, sums, terms):
             v0, v1 = P * groups[0], P * (groups[-1] + 1)
-            sums = {g: psum.tile([P, P], F32, name=f"sum{g}", tag=f"sum{g}") for g in groups}
             for d in range(D + 1):
-                term = ring.tile([P, v1 - v0], F32, name="term")
+                term = terms[d]
                 nc.vector.tensor_tensor(
-                    term[:], h_t[c][:].indirect(lists[d][:, v0 // 16 : v1 // 16]), factors[d][:, v0:v1], MULT
+                    term, h_t[c][:].indirect(lists[d][:, v0 // 16 : v1 // 16]), factors[d][:, v0:v1], MULT
                 )
                 for g in groups:
                     nc.tensor.matmul(
-                        sums[g][:],
+                        sums[g],
                         lhsT=term[:, P * g - v0 : P * (g + 1) - v0],
                         rhs=ident[:],
                         is_transpose=True,
                         start=(d == 0),
                         stop=(d == D),
                     )
-            for g, eng in zip(groups, engines):
-                dst = z_bf[g][:, :, 32 * c : 32 * (c + 1), :]
-                src = sums[g][:].rearrange("v (q u e) -> v u q e", u=2, e=2)
-                if eng == "scalar":
-                    nc.scalar.activation(dst, src, COPY, scale=-1.0)
-                else:
-                    nc.vector.tensor_scalar_mul(dst, src, -1.0)
+
+        def round_z(g, c0, c1, sums):
+            dst = z_bf[g][:, :, 32 * c0 : 32 * c1, :]
+            src = sums.rearrange("v (q u e) -> v u q e", u=2, e=2)
+            nc.scalar.activation(dst, src, COPY, scale=-1.0)
 
         def second_layer(g, engines):
             words = z_bf[g][:].rearrange("v u q e -> v (u q e)").bitcast(F32)
-            turned = psum.tile([P, 2, P], F32, name="turned", tag=f"sum{g}")
+            turned = psum.tile([P, 2, P], F32, name="turned", tag=f"early{g}")
             for u in range(2):
                 nc.tensor.transpose(turned[:, u, :], words[:, P * u : P * (u + 1)], ident[:])
             z_in = keep.tile([P, P, 2], F32, name=f"z_in{g}", align_bytes=64)
@@ -201,9 +200,9 @@ def tile_picked_lapl_silu_e_kernel(
                 in_=z_in[:].rearrange("p v u -> p (v u)").bitcast(BF16),
             )
             for m in range(2):
-                acc = psum.tile([P, P], F32, name="acc", tag="mm")
+                acc = banks[m][:, P * g : P * (g + 1)]
                 nc.tensor.matmul_mx(
-                    out=acc[:],
+                    out=acc,
                     lhsT=w2_w[:, 2 * P * m : 2 * P * (m + 1)].bitcast(FP4X4),
                     lhsT_scale=w2_sc[:, P * m : P * (m + 1)],
                     rhs=z_codes[:].bitcast(FP8X4),
@@ -212,21 +211,34 @@ def tile_picked_lapl_silu_e_kernel(
                     stop=True,
                 )
                 res = keep.tile([P, P], F32, name=f"res{g}{m}")
-                move(engines[1 + m], res[:], acc[:])
-                queue = nc.sync if m == 0 else nc.scalar
+                move(engines[1 + m], res[:], acc)
+                queue = nc.scalar if (g, m) == (1, 1) else nc.sync
                 queue.dma_start(out[P * m : P * (m + 1), P * g : P * (g + 1)], res[:])
 
-        for s0, s1 in pieces:
-            first_layer(0, s0, s1)
-        quant_w1(1, 2)
-        first_layer(1, 0, S)
-        laplacian(0, (0, 1), ("scalar", "scalar"))
-        quant_w1(2, 4)
-        first_layer(2, 0, S)
-        first_layer(3, 0, S)
-        laplacian(1, (0, 1), ("scalar", "scalar"))
-        laplacian(2, (0, 1), ("scalar", "scalar"))
-        laplacian(3, (0,), ("scalar",))
-        laplacian(3, (1,), ("scalar",))
+        for i, (s0, s1) in enumerate(pieces):
+            first_layer(0, s0, s1, i % 3)
+        first_layer(1, 0, S, 1)
+        early = [psum.tile([P, 3 * P], F32, name=f"early{g}", tag=f"early{g}") for g in range(2)]
+        late = [psum.tile([P, P], F32, name=f"late{g}", tag=f"late{g}") for g in range(2)]
+
+        def part(c):
+            return [early[g][:, P * c : P * (c + 1)] for g in range(2)]
+
+        ring_tiles = [keep.tile([P, V], F32, name=f"ring{i}") for i in range(3)]
+        ring = [t[:] for t in ring_tiles]
+        shared = keep.tile([P, 3 * V], F32, name="shared", align_bytes=64)
+        held = [shared[:, V * d : V * (d + 1)] for d in range(3)]
+        laplacian(0, (0, 1), part(0), [held[1], ring[0], ring[1], ring[2], ring[0]])
+        quant_w1(2, 4, shared[:].bitcast(BF16)[:, V : V + 8 * P])
+        first_layer(2, 0, S, 0)
+        first_layer(3, 0, S, 2)
+        laplacian(1, (0, 1), part(1), [ring[1], held[0], held[1], held[2], held[0]])
+        laplacian(2, (0, 1), part(2), [ring[2], ring[0], ring[1], held[1], held[2]])
+        for g in range(2):
+            round_z(g, 0, 3, early[g][:])
+        halves = [t[:, P * j : P * (j + 1)] for t in (ring[1], held[1]) for j in range(2)]
+        for g in range(2):
+            laplacian(3, (g,), [t[:] for t in late], [halves[((D + 1) * g + d) % 4] for d in range(D + 1)])
+            round_z(g, 3, 4, late[g][:])
         second_layer(0, ("scalar", "scalar", "scalar"))
         second_layer(1, ("scalar", "vector", "scalar"))

@@ -15,6 +15,7 @@ U8 = mybir.dt.uint8
 FP8X4 = mybir.dt.float8_e4m3fn_x4
 FP4X4 = mybir.dt.float4_e2m1fn_x4
 MULT = mybir.AluOpType.mult
+SUB = mybir.AluOpType.subtract
 SILU = mybir.ActivationFunctionType.Silu
 COPY = mybir.ActivationFunctionType.Copy
 
@@ -69,23 +70,21 @@ def tile_picked_lapl_silu_e_kernel(
                 if offs_t is None:
                     offs_t = load_list("offs", offs)
         w1_view = w1.rearrange("(p j) h -> p j h", j=4)
-        w1_raw = {}
+        w1_raw = []
 
-        def load_w1(c0, c1):
-            raw = keep.tile([P, 4, P * (c1 - c0)], F32, name=f"w1_raw{c0}", tag=f"w1_raw{c0}")
-            nc.sync.dma_start(raw[:], w1_view[:, :, P * c0 : P * c1])
-            for c in range(c0, c1):
-                w1_raw[c] = raw[:, :, P * (c - c0) : P * (c - c0 + 1)]
+        def load_w1(half):
+            raw = keep.tile([P, 4, H // 2], F32, name=f"w1_raw{half}", tag=f"w1_raw{half}")
+            nc.sync.dma_start(raw[:], w1_view[:, :, half * (H // 2) : (half + 1) * (H // 2)])
+            w1_raw.append(raw[:].rearrange("p j (q t) -> p q t j", t=4))
 
-        load_w1(0, 1)
-        load_w1(1, 2)
+        load_w1(0)
+        load_w1(1)
         cen_t = load_list("cen", cen)
         pos_t = [load_list("pos1", pos1)]
         gate_all = keep.tile([P, D, V], F32, name="gate_all")
         nc.sync.dma_start(gate_all[:], gate.rearrange("d p v -> p d v"))
         gate_t = [gate_all[:, d, :] for d in range(D)]
         pos_t.extend(load_list(name, ap) for name, ap in (("pos2", pos2), ("pos3", pos3), ("pos4", pos4)))
-        load_w1(2, 4)
         w2_w = keep.tile([P, 2 * N], U8, name="w2_w", align_bytes=64)
         nc.sync.dma_start(w2_w[:].bitcast(I32), w2_words[0].bitcast(I32))
         for q in range(4):
@@ -112,27 +111,32 @@ def tile_picked_lapl_silu_e_kernel(
         w1_codes = keep.tile([P, H], U32, name="w1_codes", align_bytes=64)
         w1_sc = keep.tile([P, H], U8, name="w1_sc", align_bytes=64)
 
-        def cast_w1(c):
-            src = w1_raw[c]
-            return src.rearrange("p j (c i) -> p c j i", i=4)
-
         def quant_w1(c0, c1, bf):
-            for c in range(c0, c1):
-                nc.scalar.copy(
-                    bf[:, 4 * P * (c - c0) : 4 * P * (c - c0 + 1)].rearrange("p (c i j) -> p c j i", i=4, j=4),
-                    cast_w1(c),
-                )
             nc.vector.quantize_mx(
                 out=w1_codes[:, P * c0 : P * c1].bitcast(FP8X4), scales=w1_sc[:, P * c0 : P * c1], in_=bf
             )
+
+        def low_pair(half):
+            bf = keep.tile([P, 4 * P], BF16, name=f"w1_low{half}", align_bytes=64)
+            nc.scalar.copy(
+                bf[:].rearrange("p (q t j) -> p q j t", t=2, j=4),
+                w1_raw[half][:, :, 0:2, :].rearrange("p q t j -> p q j t"),
+            )
+            quant_w1(half, half + 1, bf[:])
+
+        def high_pair(bf):
+            dealt = bf.rearrange("p (t q j) -> p q t j", t=2, j=4)
+            for half in range(2):
+                nc.scalar.copy(dealt[:, 64 * half : 64 * (half + 1), :, :], w1_raw[half][:, :, 2:4, :])
+            quant_w1(2, 4, bf)
 
         x_codes = keep.tile([P, S], U32, name="x_codes", align_bytes=64)
         x_sc = keep.tile([P, S], U8, name="x_sc", align_bytes=64)
         picked_bf = picked[:].rearrange("p s u -> p (s u)").bitcast(BF16)
         pieces = [(s0, s0 + S // 2) for s0 in range(0, S, S // 2)]
-        nc.vector.tensor_copy(picked[:, :, 1], pairs[1][:].indirect(offs_t[:]))
-        w1_first = keep.tile([P, 4 * P], BF16, name="w1_first", align_bytes=64)
-        quant_w1(0, 1, w1_first[:])
+        for s0, s1 in pieces:
+            nc.vector.tensor_copy(picked[:, s0:s1, 1], pairs[1][:].indirect(offs_t[:, s0 // 16 : s1 // 16]))
+        low_pair(0)
         for s0, s1 in pieces:
             nc.vector.quantize_mx(
                 out=x_codes[:, s0:s1].bitcast(FP8X4),
@@ -140,9 +144,8 @@ def tile_picked_lapl_silu_e_kernel(
                 in_=picked_bf[:, 4 * s0 : 4 * s1],
             )
 
-        w1_second = keep.tile([P, 4 * P], BF16, name="w1_second", align_bytes=64)
-        quant_w1(1, 2, w1_second[:])
-        h_t = [keep.tile([P, S], F32, name=f"h{c}", tag="w1_raw1" if c == 0 else f"h{c}") for c in range(4)]
+        low_pair(1)
+        h_t = [keep.tile([P, S], F32, name=f"h{c}") for c in range(4)]
 
         banks = [psum.tile([P, S], F32, name=f"bank{b}") for b in range(3)]
 
@@ -180,24 +183,23 @@ def tile_picked_lapl_silu_e_kernel(
                         stop=(d == D),
                     )
 
-        def round_z(g, c0, c1, sums):
-            dst = z_bf[g][:, :, 32 * c0 : 32 * c1, :]
-            src = sums.rearrange("v (q u e) -> v u q e", u=2, e=2)
+        def round_z(dst, src):
             nc.scalar.activation(dst, src, COPY, scale=-1.0)
 
+        def turn(g, u):
+            words = z_bf[g][:, u, :, :].rearrange("v q e -> v (q e)").bitcast(F32)
+            nc.tensor.transpose(turned[g][:, u, :], words, ident[:])
+
+        def weave(g):
+            nc.scalar.copy(z_in[g][:], turned[g][:].rearrange("p u v -> p v u"))
+
         def second_layer(g, engines):
-            words = z_bf[g][:].rearrange("v u q e -> v (u q e)").bitcast(F32)
-            turned = psum.tile([P, 2, P], F32, name="turned", tag=f"early{g}")
-            for u in range(2):
-                nc.tensor.transpose(turned[:, u, :], words[:, P * u : P * (u + 1)], ident[:])
-            z_in = keep.tile([P, P, 2], F32, name=f"z_in{g}", align_bytes=64)
-            move(engines[0], z_in[:], turned[:].rearrange("p u v -> p v u"))
             z_codes = keep.tile([P, P], U32, name=f"z_codes{g}", align_bytes=64)
             z_sc = keep.tile([P, P], U8, name=f"z_sc{g}", align_bytes=64)
             nc.vector.quantize_mx(
                 out=z_codes[:].bitcast(FP8X4),
                 scales=z_sc[:],
-                in_=z_in[:].rearrange("p v u -> p (v u)").bitcast(BF16),
+                in_=z_in[g][:].rearrange("p v u -> p (v u)").bitcast(BF16),
             )
             for m in range(2):
                 acc = banks[m][:, P * g : P * (g + 1)]
@@ -211,34 +213,60 @@ def tile_picked_lapl_silu_e_kernel(
                     stop=True,
                 )
                 res = keep.tile([P, P], F32, name=f"res{g}{m}")
-                move(engines[1 + m], res[:], acc)
+                move(engines[m], res[:], acc)
                 queue = nc.scalar if (g, m) == (1, 1) else nc.sync
                 queue.dma_start(out[P * m : P * (m + 1), P * g : P * (g + 1)], res[:])
 
         for i, (s0, s1) in enumerate(pieces):
             first_layer(0, s0, s1, i % 3)
         first_layer(1, 0, S, 1)
-        early = [psum.tile([P, 3 * P], F32, name=f"early{g}", tag=f"early{g}") for g in range(2)]
-        late = [psum.tile([P, P], F32, name=f"late{g}", tag=f"late{g}") for g in range(2)]
+        early = [psum.tile([P, 2 * P], F32, name=f"early{g}", tag=f"early{g}") for g in range(2)]
+        late = [psum.tile([P, 2 * P], F32, name=f"late{g}", tag=f"late{g}") for g in range(2)]
+        z_in = [keep.tile([P, P, 2], F32, name=f"z_in{g}", align_bytes=64) for g in range(2)]
 
         def part(c):
-            return [early[g][:, P * c : P * (c + 1)] for g in range(2)]
+            return [(early, late)[c // 2][g][:, P * (c % 2) : P * (c % 2 + 1)] for g in range(2)]
 
-        ring_tiles = [keep.tile([P, V], F32, name=f"ring{i}") for i in range(3)]
-        ring = [t[:] for t in ring_tiles]
-        shared = keep.tile([P, 3 * V], F32, name="shared", align_bytes=64)
-        held = [shared[:, V * d : V * (d + 1)] for d in range(3)]
-        laplacian(0, (0, 1), part(0), [held[1], ring[0], ring[1], ring[2], ring[0]])
-        quant_w1(2, 4, shared[:].bitcast(BF16)[:, V : V + 8 * P])
+        def fresh(name, count, width, tag=None):
+            tile = keep.tile([P, count, width], F32, name=name, tag=tag or name)
+            return [tile[:, i, :] for i in range(count)]
+
+        first_term = keep.tile([P, V], F32, name="first_term", tag="w1_rest", align_bytes=64)
+        terms0 = fresh("terms0", D, V)
+        laplacian(0, (0, 1), part(0), [first_term[:]] + terms0)
+        w1_rest = keep.tile([P, 8 * P], BF16, name="w1_rest", tag="w1_rest", align_bytes=64)
+        high_pair(w1_rest[:])
         first_layer(2, 0, S, 0)
-        first_layer(3, 0, S, 2)
-        laplacian(1, (0, 1), part(1), [ring[1], held[0], held[1], held[2], held[0]])
-        laplacian(2, (0, 1), part(2), [ring[2], ring[0], ring[1], held[1], held[2]])
+        first_layer(3, 0, S, 0)
+        laplacian(1, (0, 1), part(1), terms0[:1] + fresh("terms1", D, V, "w1_raw1"))
         for g in range(2):
-            round_z(g, 0, 3, early[g][:])
-        halves = [t[:, P * j : P * (j + 1)] for t in (ring[1], held[1]) for j in range(2)]
+            round_z(z_bf[g][:, 0, :, :].rearrange("v q e -> v (q e)"), early[g][:])
+        turned = [psum.tile([P, 2, P], F32, name=f"turned{g}", tag=f"early{g}") for g in range(2)]
+        laplacian(2, (0,), part(2), fresh("terms20", D + 1, P))
         for g in range(2):
-            laplacian(3, (g,), [t[:] for t in late], [halves[((D + 1) * g + d) % 4] for d in range(D + 1)])
-            round_z(g, 3, 4, late[g][:])
-        second_layer(0, ("scalar", "scalar", "scalar"))
-        second_layer(1, ("scalar", "vector", "scalar"))
+            turn(g, 0)
+        laplacian(3, (0,), part(3), fresh("terms30", D + 1, P))
+        round_z(z_bf[0][:, 1, :, :], late[0][:].rearrange("v (e q) -> v q e", e=2))
+        turn(0, 1)
+        weave(0)
+        laplacian(2, (1,), part(2), fresh("terms21", D + 1, P))
+        second_layer(0, ("scalar", "scalar"))
+        round_z(z_bf[1][:, 1, :, :], late[1][:, 0:P].unsqueeze(2).to_broadcast([P, P, 2]))
+        turn(1, 1)
+        weave(1)
+
+        a1, a2, a3, a4, b1, b2, b3 = fresh("direct", 7, P)
+
+        def looked_up(d):
+            return h_t[3][:].indirect(lists[d][:, P // 16 : V // 16])
+
+        nc.vector.tensor_tensor(a1, looked_up(1), factors[1][:, P:V], MULT)
+        nc.vector.tensor_tensor(a2, looked_up(2), factors[2][:, P:V], MULT)
+        nc.vector.tensor_tensor(b1, looked_up(0), a1, SUB)
+        nc.vector.tensor_tensor(a3, looked_up(3), factors[3][:, P:V], MULT)
+        nc.vector.tensor_tensor(b2, b1, a2, SUB)
+        nc.vector.tensor_tensor(a4, looked_up(4), factors[4][:, P:V], MULT)
+        nc.vector.tensor_tensor(b3, b2, a3, SUB)
+        slots = z_in[1][:].rearrange("p v u -> p (v u)").bitcast(BF16).rearrange("p (v t) -> p v t", t=4)
+        nc.vector.tensor_tensor(slots[:, :, 3], b3, a4, SUB)
+        second_layer(1, ("vector", "scalar"))

from contextlib import ExitStack

import concourse.mybir as mybir
from concourse.masks import make_identity

K, T, S, D, V, H, N = 512, 1024, 512, 4, 256, 512, 256
FLOPS = 2 * K * H * S + 2 * H * N * V

F32 = mybir.dt.float32
BF16 = mybir.dt.bfloat16
I32 = mybir.dt.int32
U32 = mybir.dt.uint32
U16 = mybir.dt.uint16
U8 = mybir.dt.uint8
FP8X4 = mybir.dt.float8_e4m3fn_x4
FP4X4 = mybir.dt.float4_e2m1fn_x4
MULT = mybir.AluOpType.mult
SUB = mybir.AluOpType.subtract
SILU = mybir.ActivationFunctionType.Silu
COPY = mybir.ActivationFunctionType.Copy

P = 128
X_CHUNKS = (
    ((0, 640, "scalar"), (640, 1024, "vector")),
    ((0, 384, "scalar"), (384, 768, "scalar"), (768, 1024, "vector")),
)
W1_CHUNKS = ((0, 1), (1, 2), (2, 4))


def tile_picked_lapl_silu_e_kernel(
    tc, xT, w1, w2_words, w2_scales, gate, offs, cen, pos1, pos2, pos3, pos4, out
):
    nc = tc.nc

    def move(engine, dst, src):
        if engine == "scalar":
            nc.scalar.copy(dst, src)
        else:
            nc.vector.tensor_copy(dst, src)

    with ExitStack() as ctx:
        keep = ctx.enter_context(tc.tile_pool(name="keep", bufs=1))
        psum = ctx.enter_context(tc.psum_pool(name="psum", bufs=1))

        def load_list(name, ap):
            tile = keep.tile(list(ap.shape), U16, name=name)
            nc.sync.dma_start(tile[:], ap)
            return tile

        warm = keep.tile([P, 8], F32, name="warm")
        warm_out = keep.tile([P, 8], F32, name="warm_out")
        nc.vector.memset(warm[:], 0.0)
        nc.scalar.activation(warm_out[:], warm[:], SILU)

        ident = keep.tile([P, P], F32, name="ident")
        make_identity(nc, ident[:])
        minus_one = keep.tile([P, V], F32, name="minus_one")
        nc.vector.memset(minus_one[:], -1.0)
        w2_sc = keep.tile([P, N], U8, name="w2_sc", align_bytes=64)
        nc.vector.memset(w2_sc[:].bitcast(I32), 0)

        x_view = xT.rearrange("(p u e) t -> p u e t", u=2, e=2)
        x_raw = {}
        offs_t = None
        for u in range(2):
            for c0, c1, eng in X_CHUNKS[u]:
                raw = keep.tile([P, 2, c1 - c0], F32, name=f"x_raw{u}_{c0}")
                nc.sync.dma_start(raw[:], x_view[:, u, :, c0:c1])
                x_raw[u, c0] = raw
                if offs_t is None:
                    offs_t = load_list("offs", offs)
        w1_view = w1.rearrange("(p j) h -> p j h", j=4)
        w1_raw = []

        def load_w1(half):
            raw = keep.tile([P, 4, H // 2], F32, name=f"w1_raw{half}", tag=f"w1_raw{half}")
            nc.sync.dma_start(raw[:], w1_view[:, :, half * (H // 2) : (half + 1) * (H // 2)])
            w1_raw.append(raw[:].rearrange("p j (q t) -> p q t j", t=4))

        load_w1(0)
        load_w1(1)
        cen_t = load_list("cen", cen)
        pos_t = [load_list("pos1", pos1)]
        gate_all = keep.tile([P, D, V], F32, name="gate_all")
        nc.sync.dma_start(gate_all[:], gate.rearrange("d p v -> p d v"))
        gate_t = [gate_all[:, d, :] for d in range(D)]
        pos_t.extend(load_list(name, ap) for name, ap in (("pos2", pos2), ("pos3", pos3), ("pos4", pos4)))
        w2_w = keep.tile([P, 2 * N], U8, name="w2_w", align_bytes=64)
        nc.sync.dma_start(w2_w[:].bitcast(I32), w2_words[0].bitcast(I32))
        for q in range(4):
            nc.sync.dma_start(
                w2_sc[32 * q : 32 * q + 4, :].bitcast(I32), w2_scales[0, 4 * q : 4 * q + 4, :].bitcast(I32)
            )

        picked = keep.tile([P, S, 2], U32, name="picked", align_bytes=64)
        pairs = []
        for u in range(2):
            pr = keep.tile([P, T], U32, name=f"pairs{u}", tag=f"pairs{u}", align_bytes=64)
            pr_bf = pr[:].bitcast(BF16)
            for c0, c1, eng in X_CHUNKS[u]:
                move(
                    eng,
                    pr_bf[:, 2 * c0 : 2 * c1].rearrange("p (c i e) -> p c e i", i=4, e=2),
                    x_raw[u, c0][:].rearrange("p e (c i) -> p c e i", i=4),
                )
            pairs.append(pr)
            if u == 0:
                nc.vector.tensor_copy(picked[:, :, 0], pr[:].indirect(offs_t[:]))

        w1_bf = []
        w1_codes = keep.tile([P, H], U32, name="w1_codes", align_bytes=64)
        w1_sc = keep.tile([P, H], U8, name="w1_sc", align_bytes=64)

        def quant_w1(c0, c1, bf):
            nc.vector.quantize_mx(
                out=w1_codes[:, P * c0 : P * c1].bitcast(FP8X4), scales=w1_sc[:, P * c0 : P * c1], in_=bf
            )

        def low_pair(half):
            bf = keep.tile([P, 4 * P], BF16, name=f"w1_low{half}", align_bytes=64)
            nc.scalar.copy(
                bf[:].rearrange("p (q t j) -> p q j t", t=2, j=4),
                w1_raw[half][:, :, 0:2, :].rearrange("p q t j -> p q j t"),
            )
            quant_w1(half, half + 1, bf[:])

        def high_pair(bf):
            dealt = bf.rearrange("p (t q j) -> p q t j", t=2, j=4)
            for half in range(2):
                nc.scalar.copy(dealt[:, 64 * half : 64 * (half + 1), :, :], w1_raw[half][:, :, 2:4, :])
            quant_w1(2, 4, bf)

        x_codes = keep.tile([P, S], U32, name="x_codes", align_bytes=64)
        x_sc = keep.tile([P, S], U8, name="x_sc", align_bytes=64)
        picked_bf = picked[:].rearrange("p s u -> p (s u)").bitcast(BF16)
        pieces = [(s0, s0 + S // 2) for s0 in range(0, S, S // 2)]
        for s0, s1 in pieces:
            nc.vector.tensor_copy(picked[:, s0:s1, 1], pairs[1][:].indirect(offs_t[:, s0 // 16 : s1 // 16]))
        low_pair(0)
        for s0, s1 in pieces:
            nc.vector.quantize_mx(
                out=x_codes[:, s0:s1].bitcast(FP8X4),
                scales=x_sc[:, s0:s1],
                in_=picked_bf[:, 4 * s0 : 4 * s1],
            )

        low_pair(1)
        h_t = [keep.tile([P, S], F32, name=f"h{c}") for c in range(4)]

        banks = [psum.tile([P, S], F32, name=f"bank{b}") for b in range(3)]

        def first_layer(c, s0, s1, bank):
            acc = banks[bank][:, 0 : s1 - s0]
            nc.tensor.matmul_mx(
                out=acc,
                lhsT=w1_codes[:, P * c : P * (c + 1)].bitcast(FP8X4),
                lhsT_scale=w1_sc[:, P * c : P * (c + 1)],
                rhs=x_codes[:, s0:s1].bitcast(FP8X4),
                rhs_scale=x_sc[:, s0:s1],
                start=True,
                stop=True,
            )
            nc.scalar.activation(h_t[c][:, s0:s1], acc, SILU)

        z_bf = [keep.tile([P, 2, P, 2], BF16, name=f"z_bf{g}") for g in range(2)]
        lists = [cen_t] + pos_t
        factors = [minus_one[:]] + gate_t

        def laplacian(c, groups, sums, terms):
            v0, v1 = P * groups[0], P * (groups[-1] + 1)
            for d in range(D + 1):
                term = terms[d]
                nc.vector.tensor_tensor(
                    term, h_t[c][:].indirect(lists[d][:, v0 // 16 : v1 // 16]), factors[d][:, v0:v1], MULT
                )
                for g in groups:
                    nc.tensor.matmul(
                        sums[g],
                        lhsT=term[:, P * g - v0 : P * (g + 1) - v0],
                        rhs=ident[:],
                        is_transpose=True,
                        start=(d == 0),
                        stop=(d == D),
                    )

        def round_z(dst, src):
            nc.scalar.activation(dst, src, COPY, scale=-1.0)

        def turn(g, u):
            words = z_bf[g][:, u, :, :].rearrange("v q e -> v (q e)").bitcast(F32)
            nc.tensor.transpose(turned[g][:, u, :], words, ident[:])

        def weave(g):
            nc.scalar.copy(z_in[g][:], turned[g][:].rearrange("p u v -> p v u"))

        def second_layer(g, engines):
            z_codes = keep.tile([P, P], U32, name=f"z_codes{g}", align_bytes=64)
            z_sc = keep.tile([P, P], U8, name=f"z_sc{g}", align_bytes=64)
            nc.vector.quantize_mx(
                out=z_codes[:].bitcast(FP8X4),
                scales=z_sc[:],
                in_=z_in[g][:].rearrange("p v u -> p (v u)").bitcast(BF16),
            )
            for m in range(2):
                acc = banks[m][:, P * g : P * (g + 1)]
                nc.tensor.matmul_mx(
                    out=acc,
                    lhsT=w2_w[:, 2 * P * m : 2 * P * (m + 1)].bitcast(FP4X4),
                    lhsT_scale=w2_sc[:, P * m : P * (m + 1)],
                    rhs=z_codes[:].bitcast(FP8X4),
                    rhs_scale=z_sc[:],
                    start=True,
                    stop=True,
                )
                res = keep.tile([P, P], F32, name=f"res{g}{m}")
                move(engines[m], res[:], acc)
                queue = nc.scalar if (g, m) == (1, 1) else nc.sync
                queue.dma_start(out[P * m : P * (m + 1), P * g : P * (g + 1)], res[:])

        for i, (s0, s1) in enumerate(pieces):
            first_layer(0, s0, s1, i % 3)
        first_layer(1, 0, S, 1)
        early = [psum.tile([P, 2 * P], F32, name=f"early{g}", tag=f"early{g}") for g in range(2)]
        late = [psum.tile([P, 2 * P], F32, name=f"late{g}", tag=f"late{g}") for g in range(2)]
        z_in = [keep.tile([P, P, 2], F32, name=f"z_in{g}", align_bytes=64) for g in range(2)]

        def part(c):
            return [(early, late)[c // 2][g][:, P * (c % 2) : P * (c % 2 + 1)] for g in range(2)]

        def fresh(name, count, width, tag=None):
            tile = keep.tile([P, count, width], F32, name=name, tag=tag or name)
            return [tile[:, i, :] for i in range(count)]

        first_term = keep.tile([P, V], F32, name="first_term", tag="w1_rest", align_bytes=64)
        terms0 = fresh("terms0", D, V)
        laplacian(0, (0, 1), part(0), [first_term[:]] + terms0)
        w1_rest = keep.tile([P, 8 * P], BF16, name="w1_rest", tag="w1_rest", align_bytes=64)
        high_pair(w1_rest[:])
        first_layer(2, 0, S, 0)
        first_layer(3, 0, S, 0)
        laplacian(1, (0, 1), part(1), terms0[:1] + fresh("terms1", D, V, "w1_raw1"))
        for g in range(2):
            round_z(z_bf[g][:, 0, :, :].rearrange("v q e -> v (q e)"), early[g][:])
        turned = [psum.tile([P, 2, P], F32, name=f"turned{g}", tag=f"early{g}") for g in range(2)]
        laplacian(2, (0,), part(2), fresh("terms20", D + 1, P))
        for g in range(2):
            turn(g, 0)
        laplacian(3, (0,), part(3), fresh("terms30", D + 1, P))
        round_z(z_bf[0][:, 1, :, :], late[0][:].rearrange("v (e q) -> v q e", e=2))
        turn(0, 1)
        weave(0)
        laplacian(2, (1,), part(2), fresh("terms21", D + 1, P))
        second_layer(0, ("scalar", "scalar"))
        round_z(z_bf[1][:, 1, :, :], late[1][:, 0:P].unsqueeze(2).to_broadcast([P, P, 2]))
        turn(1, 1)
        weave(1)

        a1, a2, a3, a4, b1, b2, b3 = fresh("direct", 7, P)

        def looked_up(d):
            return h_t[3][:].indirect(lists[d][:, P // 16 : V // 16])

        nc.vector.tensor_tensor(a1, looked_up(1), factors[1][:, P:V], MULT)
        nc.vector.tensor_tensor(a2, looked_up(2), factors[2][:, P:V], MULT)
        nc.vector.tensor_tensor(b1, looked_up(0), a1, SUB)
        nc.vector.tensor_tensor(a3, looked_up(3), factors[3][:, P:V], MULT)
        nc.vector.tensor_tensor(b2, b1, a2, SUB)
        nc.vector.tensor_tensor(a4, looked_up(4), factors[4][:, P:V], MULT)
        nc.vector.tensor_tensor(b3, b2, a3, SUB)
        slots = z_in[1][:].rearrange("p v u -> p (v u)").bitcast(BF16).rearrange("p (v t) -> p v t", t=4)
        nc.vector.tensor_tensor(slots[:, :, 3], b3, a4, SUB)
        second_layer(1, ("vector", "scalar"))
